import numpy as np
CORES = [61,69,101,62,70,102]
N = 6
R, T = 1024, 32
def entries(a): return a.T.reshape(-1)
def pack(v, P): return np.ascontiguousarray(np.asarray(v, np.int32).reshape(-1, P).T)
def lists(rng, how):
    Q = rng.permutation(N * R)[:N * T]
    if how == "hotrank": Q = R * int(rng.integers(N)) + rng.permutation(R)[:N * T]
    if how == "own": Q = np.concatenate([R * r + rng.permutation(R)[:T] for r in range(N)])
    if how == "sorted": Q = np.sort(Q)
    if how == "edge":
        ends = np.concatenate([R * np.arange(N), R * np.arange(N) + R - 1]); rest = np.setdiff1d(rng.permutation(N * R), ends, assume_unique=True)
        Q = rng.permutation(np.concatenate([ends, rng.permutation(rest)[:N * T - 2 * N]]))
    return {"pos": np.stack([pack(q, 16) for q in Q.reshape(N, T)])}
def setup_inputs(rng):
    return dict({"tab": rng.standard_normal((N, 128, R), dtype=np.float32), "new": rng.standard_normal((N, 128, T), dtype=np.float32)}, **lists(rng, "uniform"))
def setup_inputs_edge(rng):
    d = setup_inputs(rng); d.update(lists(rng, "edge"))
    for k in ("tab", "new"): d[k] = (d[k].astype(np.float32) * 1048576.0).astype(d[k].dtype)
    return d
def setup_inputs_hotrank(rng):
    d = setup_inputs(rng); d.update(lists(rng, "hotrank"))
    for k in ("tab", "new"): d[k] = (d[k].astype(np.float32) * (1 / 1024.0)).astype(d[k].dtype)
    return d
def setup_inputs_own(rng):
    d = setup_inputs(rng); d.update(lists(rng, "own"))
    return d
def setup_inputs_sorted(rng):
    d = setup_inputs(rng); d.update(lists(rng, "sorted"))
    return d
def check_inputs(x):
    bad = []
    if x["pos"].min() < 0 or x["pos"].max() >= N * R: bad.append("pos out of range")
    if len(np.unique(x["pos"])) != x["pos"].size: bad.append("a place is named twice")
    return bad
def reference(tab, new, pos):
    A = np.concatenate(list(tab), axis=1)
    for r in range(N): A[:, entries(pos[r])] = new[r]
    return {"y": np.stack([A[:, R * r:R * r + R] for r in range(N)])}

@@ -1,0 +1,122 @@
+import comms_topo
+from concourse.bass import DstId, RemoteDMATransfer
+from concourse.mybir import AluOpType
+
+CORES = [61, 69, 101, 62, 70, 102]
+N, R, NEW = 6, 1024, 32
+HALF = NEW + 4
+WIDE = 2 * HALF
+NCHIPS = len(set(comms_topo.chip(c) for c in CORES))
+
+SCRATCH = {
+    "win": ("sbuf", [128, N * R], "float32"),
+    "posi": ("sbuf", [16, 2], "int32"),
+    "posf": ("sbuf", [16, 4], "float32"),
+    "rep": ("sbuf", [16, 128], "float32"),
+    "ps": ("psum", [128, 4], "float32"),
+}
+SEMAPHORES = ["ones", "rep", "pos", "posf", "mm", "msg", "new", "tab", "cv", "sc", "sent", "out"]
+for _k in range(NCHIPS):
+    SCRATCH["blk%d" % _k] = ("sbuf", [128, WIDE], "float32")
+    SCRATCH["off%d" % _k] = ("sbuf", [128, 4], "uint16")
+    SEMAPHORES.append("arr%d" % _k)
+
+
+def _layout(cores, topo):
+    chips = sorted(set(topo.chip(c) for c in cores))
+    members = [[c for c in cores if topo.chip(c) == ch] for ch in chips]
+    fwd = {c: [] for c in cores}
+    for i, src in enumerate(members):
+        todo = [j for j in range(len(members)) if j != i]
+        able = {j: [c for c in src if all(topo.may_write(c, d) for d in members[j])] for j in todo}
+        for j in sorted(todo, key=lambda j: len(able[j])):
+            f = min(able[j], key=lambda c: len(fwd[c]))
+            fwd[f] += members[j]
+    return chips, members, fwd
+
+
+def _engines(c, cores, topo):
+    m = None
+    for d in cores:
+        if d != c:
+            m = topo.mask(c, d) if m is None else m & topo.mask(c, d)
+    return m, bin(m).count("1")
+
+
+def rank_program(g, core, T, topo):
+    rank = T.rank_of(core)
+    if rank is None:
+        return
+    cores = list(T.cores)
+    chips, members, fwd = _layout(cores, topo)
+    ci = chips.index(topo.chip(core))
+    side = members[ci].index(core)
+    partner = members[ci][1 - side]
+    S = T.sem
+    mine = T["blk%d" % ci]
+    lo = side * HALF
+    newc = 0 if side == 0 else HALF + 4
+    posc = NEW if side == 0 else HALF
+    c0 = rank * R
+    mask, ne = _engines(core, cores, topo)
+
+    g.scalar.dma_start(T.posi[:, :], T.pos[:, :]).then_inc(S.pos, 16)
+    g.sync.dma_start(mine[:, newc:newc + NEW], T.new[:, :]).then_inc(S.new, 16)
+    g.sync.dma_start(T.win[:, c0:c0 + R], T.tab[:, :]).then_inc(S.tab, 16)
+
+    g.vector.memset(T.rep[:, :], 1.0).then_inc(S.ones, 1)
+    g.wait_ge(S.ones, 1)
+    g.affine_select(T.rep[:, :], T.rep[:, :], [[0, 8], [-1, 16]], AluOpType.is_equal, 0.0, 0, 1).then_inc(S.rep, 1)
+
+    pc = 2 if side == 0 else 0
+    g.vector.memset(T.posf[:, 2 - pc:4 - pc], 0.0).then_inc(S.posf, 1)
+    g.vector.wait_ge(S.pos, 16)
+    g.vector.tensor_copy(T.posf[:, pc:pc + 2], T.posi[:, :]).then_inc(S.posf, 1)
+    g.tensor.wait_ge(S.rep, 1)
+    g.tensor.wait_ge(S.posf, 2)
+    g.tensor.matmul(T.ps[:, :], T.rep[:, :], T.posf[:, :], start=True, stop=True).then_inc(S.mm, 1)
+    g.vector.wait_ge(S.mm, 1)
+    g.vector.tensor_copy(mine[:, posc:posc + 4], T.ps[:, :]).then_inc(S.msg, 1)
+
+    g.wait_ge(S.new, 16)
+    g.wait_ge(S.msg, 1)
+    rid, pid, _se = topo.addr(partner)
+    g.remote_dma(out_ap=mine[:, lo:lo + HALF], in_ap=mine[:, lo:lo + HALF], remote_sem=S["arr%d" % ci],
+                 local_sem=S.sent, pid=pid, routing_id=rid, dma_engine_mask=mask)
+    sent = ne
+    half_in = _engines(partner, cores, topo)[1]
+
+    if fwd[core]:
+        g.wait_ge(S["arr%d" % ci], half_in)
+        ids = [DstId(rid=topo.addr(d)[0], pnc=topo.addr(d)[1]) for d in fwd[core]]
+        g.remote_dma_fused([RemoteDMATransfer(dst_ids=ids, dma_engine_mask=mask, remote_sem=S["arr%d" % ci],
+                                              srcs=[mine[:, :]], dsts=[mine[:, :] for _d in ids])],
+                           local_sem=S.sent)
+        sent += ne
+
+    others = [j for j in range(len(chips)) if j != ci]
+    others.sort(key=lambda j: 0 if topo.same_plane(chips[ci], chips[j]) else 1)
+    v = g.vector
+    ncv = nsc = 0
+    for j in [ci] + others:
+        blk, off = T["blk%d" % j], T["off%d" % j]
+        if j == ci:
+            v.wait_ge(S.msg, 1)
+            v.wait_ge(S.new, 16)
+            v.wait_ge(S.tab, 16)
+            v.wait_ge(S["arr%d" % j], half_in)
+        else:
+            sender = [c for c in members[j] if core in fwd[c]][0]
+            v.wait_ge(S["arr%d" % j], _engines(sender, cores, topo)[1])
+        v.tensor_copy(off[:, :], blk[:, HALF - 2:HALF + 2]).then_inc(S.cv, 1)
+        ncv += 1
+        v.wait_ge(S.cv, ncv)
+        for oc, dc in ((0, 0), (2, HALF + 4)):
+            v.wait_ge(S.sc, nsc)
+            v.tensor_copy(T.win[:, 0:N * R].indirect(off[:, oc:oc + 2]), blk[:, dc:dc + NEW]).then_inc(S.sc, 1)
+            nsc += 1
+
+    g.sync.wait_ge(S.sc, nsc)
+    g.sync.dma_start(T.y[:, :], T.win[:, c0:c0 + R]).then_inc(S.out, 16)
+    g.sync.wait_ge(S.out, 16)
+    g.wait_ge(S.sent, sent)

@@ -19,7 +19,7 @@ SEMAPHORES = ["ones", "rep", "pos", "posf", "mm", "msg", "new", "tab", "cv", "sc
 for _k in range(NCHIPS):
     SCRATCH["blk%d" % _k] = ("sbuf", [128, WIDE], "float32")
     SCRATCH["off%d" % _k] = ("sbuf", [128, 4], "uint16")
-    SEMAPHORES.append("arr%d" % _k)
+    SEMAPHORES += ["arr%d_0" % _k, "arr%d_1" % _k]
 
 
 def _layout(cores, topo):
@@ -54,11 +54,16 @@ def rank_program(g, core, T, topo):
     partner = members[ci][1 - side]
     S = T.sem
     mine = T["blk%d" % ci]
-    lo = side * HALF
     newc = 0 if side == 0 else HALF + 4
     posc = NEW if side == 0 else HALF
     c0 = rank * R
     mask, ne = _engines(core, cores, topo)
+
+    def alone(f):
+        return bool(fwd[f]) and not fwd[members[chips.index(topo.chip(f))][1 - members[chips.index(topo.chip(f))].index(f)]]
+
+    def entry(f, d):
+        return members[chips.index(topo.chip(d))].index(d) == members[chips.index(topo.chip(f))].index(f)
 
     g.scalar.dma_start(T.posi[:, :], T.pos[:, :]).then_inc(S.pos, 16)
     g.sync.dma_start(mine[:, newc:newc + NEW], T.new[:, :]).then_inc(S.new, 16)
@@ -78,45 +83,65 @@ def rank_program(g, core, T, topo):
     g.vector.wait_ge(S.mm, 1)
     g.vector.tensor_copy(mine[:, posc:posc + 4], T.ps[:, :]).then_inc(S.msg, 1)
 
+    sent = [0]
+
+    def send(j, s, dests):
+        ap = T["blk%d" % j][:, s * HALF:(s + 1) * HALF]
+        ids = [DstId(rid=topo.addr(d)[0], pnc=topo.addr(d)[1]) for d in dests]
+        g.remote_dma_fused([RemoteDMATransfer(dst_ids=ids, dma_engine_mask=mask, remote_sem=S["arr%d_%d" % (j, s)],
+                                              srcs=[ap], dsts=[ap for _d in ids])], local_sem=S.sent)
+        sent[0] += ne
+
+    todo = [(0, ci, side, None), (1, ci, 1 - side, partner)]
+    passes = []
+    for j in range(len(chips)):
+        if j != ci:
+            f = [c for c in members[j] if core in fwd[c]][0]
+            sf = members[j].index(f)
+            near = topo.same_plane(chips[ci], chips[j])
+            if not alone(f) or entry(f, core):
+                todo.append((2, j, sf, f))
+                if alone(f):
+                    passes.append((j, sf, f))
+            else:
+                todo.append((4, j, sf, partner))
+            todo.append((3 if near else 5, j, 1 - sf, f))
+
     g.wait_ge(S.new, 16)
     g.wait_ge(S.msg, 1)
-    rid, pid, _se = topo.addr(partner)
-    g.remote_dma(out_ap=mine[:, lo:lo + HALF], in_ap=mine[:, lo:lo + HALF], remote_sem=S["arr%d" % ci],
-                 local_sem=S.sent, pid=pid, routing_id=rid, dma_engine_mask=mask)
-    sent = ne
-    half_in = _engines(partner, cores, topo)[1]
-
+    early = [d for d in fwd[core] if not alone(core) or entry(core, d)]
+    if alone(core):
+        send(ci, side, early)
+        send(ci, side, [partner])
+    else:
+        send(ci, side, [partner])
+        if early:
+            send(ci, side, early)
     if fwd[core]:
-        g.wait_ge(S["arr%d" % ci], half_in)
-        ids = [DstId(rid=topo.addr(d)[0], pnc=topo.addr(d)[1]) for d in fwd[core]]
-        g.remote_dma_fused([RemoteDMATransfer(dst_ids=ids, dma_engine_mask=mask, remote_sem=S["arr%d" % ci],
-                                              srcs=[mine[:, :]], dsts=[mine[:, :] for _d in ids])],
-                           local_sem=S.sent)
-        sent += ne
+        g.wait_ge(S["arr%d_%d" % (ci, 1 - side)], _engines(partner, cores, topo)[1])
+        send(ci, 1 - side, fwd[core])
+    for j, s, f in passes:
+        g.wait_ge(S["arr%d_%d" % (j, s)], _engines(f, cores, topo)[1])
+        send(j, s, [partner])
 
-    others = [j for j in range(len(chips)) if j != ci]
-    others.sort(key=lambda j: 0 if topo.same_plane(chips[ci], chips[j]) else 1)
     v = g.vector
-    ncv = nsc = 0
-    for j in [ci] + others:
+    n = 0
+    for _due, j, s, sender in sorted(todo):
         blk, off = T["blk%d" % j], T["off%d" % j]
-        if j == ci:
+        if sender is None:
             v.wait_ge(S.msg, 1)
             v.wait_ge(S.new, 16)
             v.wait_ge(S.tab, 16)
-            v.wait_ge(S["arr%d" % j], half_in)
         else:
-            sender = [c for c in members[j] if core in fwd[c]][0]
-            v.wait_ge(S["arr%d" % j], _engines(sender, cores, topo)[1])
-        v.tensor_copy(off[:, :], blk[:, HALF - 2:HALF + 2]).then_inc(S.cv, 1)
-        ncv += 1
-        v.wait_ge(S.cv, ncv)
-        for oc, dc in ((0, 0), (2, HALF + 4)):
-            v.wait_ge(S.sc, nsc)
-            v.tensor_copy(T.win[:, 0:N * R].indirect(off[:, oc:oc + 2]), blk[:, dc:dc + NEW]).then_inc(S.sc, 1)
-            nsc += 1
+            v.wait_ge(S["arr%d_%d" % (j, s)], _engines(sender, cores, topo)[1])
+        v.tensor_copy(off[:, 2 * s:2 * s + 2], blk[:, HALF - 2 + 2 * s:HALF + 2 * s]).then_inc(S.cv, 1)
+        v.wait_ge(S.cv, n + 1)
+        v.wait_ge(S.sc, n)
+        dc = s * (HALF + 4)
+        v.tensor_copy(T.win[:, 0:N * R].indirect(off[:, 2 * s:2 * s + 2]), blk[:, dc:dc + NEW]).then_inc(S.sc, 1)
+        n += 1
 
-    g.sync.wait_ge(S.sc, nsc)
+    g.sync.wait_ge(S.sc, n)
     g.sync.dma_start(T.y[:, :], T.win[:, c0:c0 + R]).then_inc(S.out, 16)
     g.sync.wait_ge(S.out, 16)
-    g.wait_ge(S.sent, sent)
+    g.wait_ge(S.sent, sent[0])

@@ -35,12 +35,19 @@ def _layout(cores, topo):
     return chips, members, fwd
 
 
+def _bits(m):
+    return bin(m).count("1")
+
+
 def _engines(c, cores, topo):
-    m = None
+    out, home = None, None
     for d in cores:
         if d != c:
-            m = topo.mask(c, d) if m is None else m & topo.mask(c, d)
-    return m, bin(m).count("1")
+            m = topo.mask(c, d)
+            out = m if out is None else out & m
+            if topo.chip(d) == topo.chip(c):
+                home = m if home is None else home & m
+    return out, home & ~out
 
 
 def rank_program(g, core, T, topo):
@@ -57,13 +64,20 @@ def rank_program(g, core, T, topo):
     newc = 0 if side == 0 else HALF + 4
     posc = NEW if side == 0 else HALF
     c0 = rank * R
-    mask, ne = _engines(core, cores, topo)
+    out, home = _engines(core, cores, topo)
 
     def alone(f):
         return bool(fwd[f]) and not fwd[members[chips.index(topo.chip(f))][1 - members[chips.index(topo.chip(f))].index(f)]]
 
     def entry(f, d):
         return members[chips.index(topo.chip(d))].index(d) == members[chips.index(topo.chip(f))].index(f)
+
+    def listmask(f):
+        o, h = _engines(f, cores, topo)
+        return h if alone(f) else o
+
+    def exchanged(f):
+        return _bits(_engines(f, cores, topo)[1]) + _bits(listmask(f))
 
     g.scalar.dma_start(T.posi[:, :], T.pos[:, :]).then_inc(S.pos, 16)
     g.sync.dma_start(mine[:, newc:newc + NEW], T.new[:, :]).then_inc(S.new, 16)
@@ -85,55 +99,59 @@ def rank_program(g, core, T, topo):
 
     sent = [0]
 
-    def send(j, s, dests):
-        ap = T["blk%d" % j][:, s * HALF:(s + 1) * HALF]
+    def send(j, s, dests, mask, a=0, b=HALF):
+        ap = T["blk%d" % j][:, s * HALF + a:s * HALF + b]
         ids = [DstId(rid=topo.addr(d)[0], pnc=topo.addr(d)[1]) for d in dests]
         g.remote_dma_fused([RemoteDMATransfer(dst_ids=ids, dma_engine_mask=mask, remote_sem=S["arr%d_%d" % (j, s)],
                                               srcs=[ap], dsts=[ap for _d in ids])], local_sem=S.sent)
-        sent[0] += ne
+        sent[0] += _bits(mask)
 
-    todo = [(0, ci, side, None), (1, ci, 1 - side, partner)]
+    todo = [(0, ci, side, None), (1, ci, 1 - side, exchanged(partner))]
     passes = []
     for j in range(len(chips)):
         if j != ci:
             f = [c for c in members[j] if core in fwd[c]][0]
             sf = members[j].index(f)
             near = topo.same_plane(chips[ci], chips[j])
+            fo = _bits(_engines(f, cores, topo)[0])
             if not alone(f) or entry(f, core):
-                todo.append((2, j, sf, f))
+                todo.append((2, j, sf, fo))
                 if alone(f):
-                    passes.append((j, sf, f))
+                    passes.append((j, sf, fo))
             else:
-                todo.append((4, j, sf, partner))
-            todo.append((3 if near else 5, j, 1 - sf, f))
+                todo.append((4, j, sf, _bits(_engines(partner, cores, topo)[1])))
+            todo.append((3 if near else 5, j, 1 - sf, fo))
 
+    na, nb = newc - side * HALF, newc - side * HALF + NEW
+    la, lb = posc - side * HALF, posc - side * HALF + 4
     g.wait_ge(S.new, 16)
+    send(ci, side, [partner], home, na, nb)
     g.wait_ge(S.msg, 1)
     early = [d for d in fwd[core] if not alone(core) or entry(core, d)]
     if alone(core):
-        send(ci, side, early)
-        send(ci, side, [partner])
+        send(ci, side, early, out)
+        send(ci, side, [partner], listmask(core), la, lb)
     else:
-        send(ci, side, [partner])
+        send(ci, side, [partner], listmask(core), la, lb)
         if early:
-            send(ci, side, early)
+            send(ci, side, early, out)
     if fwd[core]:
-        g.wait_ge(S["arr%d_%d" % (ci, 1 - side)], _engines(partner, cores, topo)[1])
-        send(ci, 1 - side, fwd[core])
-    for j, s, f in passes:
-        g.wait_ge(S["arr%d_%d" % (j, s)], _engines(f, cores, topo)[1])
-        send(j, s, [partner])
+        g.wait_ge(S["arr%d_%d" % (ci, 1 - side)], exchanged(partner))
+        send(ci, 1 - side, fwd[core], out)
+    for j, s, eng in passes:
+        g.wait_ge(S["arr%d_%d" % (j, s)], eng)
+        send(j, s, [partner], home)
 
     v = g.vector
     n = 0
-    for _due, j, s, sender in sorted(todo):
+    for _due, j, s, eng in sorted(todo, key=lambda t: t[:3]):
         blk, off = T["blk%d" % j], T["off%d" % j]
-        if sender is None:
+        if eng is None:
             v.wait_ge(S.msg, 1)
             v.wait_ge(S.new, 16)
             v.wait_ge(S.tab, 16)
         else:
-            v.wait_ge(S["arr%d_%d" % (j, s)], _engines(sender, cores, topo)[1])
+            v.wait_ge(S["arr%d_%d" % (j, s)], eng)
         v.tensor_copy(off[:, 2 * s:2 * s + 2], blk[:, HALF - 2 + 2 * s:HALF + 2 * s]).then_inc(S.cv, 1)
         v.wait_ge(S.cv, n + 1)
         v.wait_ge(S.sc, n)

import comms_topo
from concourse.bass import DstId, RemoteDMATransfer
from concourse.mybir import AluOpType

CORES = [61, 69, 101, 62, 70, 102]
N, R, NEW = 6, 1024, 32
HALF = NEW + 4
WIDE = 2 * HALF
NCHIPS = len(set(comms_topo.chip(c) for c in CORES))

SCRATCH = {
    "win": ("sbuf", [128, N * R], "float32"),
    "posi": ("sbuf", [16, 2], "int32"),
    "posf": ("sbuf", [16, 4], "float32"),
    "rep": ("sbuf", [16, 128], "float32"),
    "ps": ("psum", [128, 4], "float32"),
}
SEMAPHORES = ["ones", "rep", "pos", "posf", "mm", "msg", "new", "tab", "cv", "sc", "sent", "out"]
for _k in range(NCHIPS):
    SCRATCH["blk%d" % _k] = ("sbuf", [128, WIDE], "float32")
    SCRATCH["off%d" % _k] = ("sbuf", [128, 4], "uint16")
    SEMAPHORES += ["arr%d_0" % _k, "arr%d_1" % _k]


def _layout(cores, topo):
    chips = sorted(set(topo.chip(c) for c in cores))
    members = [[c for c in cores if topo.chip(c) == ch] for ch in chips]
    fwd = {c: [] for c in cores}
    for i, src in enumerate(members):
        todo = [j for j in range(len(members)) if j != i]
        able = {j: [c for c in src if all(topo.may_write(c, d) for d in members[j])] for j in todo}
        for j in sorted(todo, key=lambda j: len(able[j])):
            f = min(able[j], key=lambda c: len(fwd[c]))
            fwd[f] += members[j]
    return chips, members, fwd


def _bits(m):
    return bin(m).count("1")


def _engines(c, cores, topo):
    out, home = None, None
    for d in cores:
        if d != c:
            m = topo.mask(c, d)
            out = m if out is None else out & m
            if topo.chip(d) == topo.chip(c):
                home = m if home is None else home & m
    return out, home & ~out


def rank_program(g, core, T, topo):
    rank = T.rank_of(core)
    if rank is None:
        return
    cores = list(T.cores)
    chips, members, fwd = _layout(cores, topo)
    ci = chips.index(topo.chip(core))
    side = members[ci].index(core)
    partner = members[ci][1 - side]
    S = T.sem
    mine = T["blk%d" % ci]
    newc = 0 if side == 0 else HALF + 4
    posc = NEW if side == 0 else HALF
    c0 = rank * R
    out, home = _engines(core, cores, topo)

    def alone(f):
        return bool(fwd[f]) and not fwd[members[chips.index(topo.chip(f))][1 - members[chips.index(topo.chip(f))].index(f)]]

    def entry(f, d):
        return members[chips.index(topo.chip(d))].index(d) == members[chips.index(topo.chip(f))].index(f)

    def listmask(f):
        o, h = _engines(f, cores, topo)
        return h if alone(f) else o

    def exchanged(f):
        return _bits(_engines(f, cores, topo)[1]) + _bits(listmask(f))

    g.scalar.dma_start(T.posi[:, :], T.pos[:, :]).then_inc(S.pos, 16)
    g.sync.dma_start(mine[:, newc:newc + NEW], T.new[:, :]).then_inc(S.new, 16)
    g.sync.dma_start(T.win[:, c0:c0 + R], T.tab[:, :]).then_inc(S.tab, 16)

    g.vector.memset(T.rep[:, :], 1.0).then_inc(S.ones, 1)
    g.wait_ge(S.ones, 1)
    g.affine_select(T.rep[:, :], T.rep[:, :], [[0, 8], [-1, 16]], AluOpType.is_equal, 0.0, 0, 1).then_inc(S.rep, 1)

    pc = 2 if side == 0 else 0
    g.vector.memset(T.posf[:, 2 - pc:4 - pc], 0.0).then_inc(S.posf, 1)
    g.vector.wait_ge(S.pos, 16)
    g.vector.tensor_copy(T.posf[:, pc:pc + 2], T.posi[:, :]).then_inc(S.posf, 1)
    g.tensor.wait_ge(S.rep, 1)
    g.tensor.wait_ge(S.posf, 2)
    g.tensor.matmul(T.ps[:, :], T.rep[:, :], T.posf[:, :], start=True, stop=True).then_inc(S.mm, 1)
    g.vector.wait_ge(S.mm, 1)
    g.vector.tensor_copy(mine[:, posc:posc + 4], T.ps[:, :]).then_inc(S.msg, 1)

    sent = [0]

    def send(j, s, dests, mask, a=0, b=HALF):
        ap = T["blk%d" % j][:, s * HALF + a:s * HALF + b]
        ids = [DstId(rid=topo.addr(d)[0], pnc=topo.addr(d)[1]) for d in dests]
        g.remote_dma_fused([RemoteDMATransfer(dst_ids=ids, dma_engine_mask=mask, remote_sem=S["arr%d_%d" % (j, s)],
                                              srcs=[ap], dsts=[ap for _d in ids])], local_sem=S.sent)
        sent[0] += _bits(mask)

    todo = [(0, ci, side, None), (1, ci, 1 - side, exchanged(partner))]
    passes = []
    for j in range(len(chips)):
        if j != ci:
            f = [c for c in members[j] if core in fwd[c]][0]
            sf = members[j].index(f)
            near = topo.same_plane(chips[ci], chips[j])
            fo = _bits(_engines(f, cores, topo)[0])
            if not alone(f) or entry(f, core):
                todo.append((2, j, sf, fo))
                if alone(f):
                    passes.append((j, sf, fo))
            else:
                todo.append((4, j, sf, _bits(_engines(partner, cores, topo)[1])))
            todo.append((3 if near else 5, j, 1 - sf, fo))

    na, nb = newc - side * HALF, newc - side * HALF + NEW
    la, lb = posc - side * HALF, posc - side * HALF + 4
    g.wait_ge(S.new, 16)
    send(ci, side, [partner], home, na, nb)
    g.wait_ge(S.msg, 1)
    early = [d for d in fwd[core] if not alone(core) or entry(core, d)]
    if alone(core):
        send(ci, side, early, out)
        send(ci, side, [partner], listmask(core), la, lb)
    else:
        send(ci, side, [partner], listmask(core), la, lb)
        if early:
            send(ci, side, early, out)
    if fwd[core]:
        g.wait_ge(S["arr%d_%d" % (ci, 1 - side)], exchanged(partner))
        send(ci, 1 - side, fwd[core], out)
    for j, s, eng in passes:
        g.wait_ge(S["arr%d_%d" % (j, s)], eng)
        send(j, s, [partner], home)

    v = g.vector
    n = 0
    for _due, j, s, eng in sorted(todo, key=lambda t: t[:3]):
        blk, off = T["blk%d" % j], T["off%d" % j]
        if eng is None:
            v.wait_ge(S.msg, 1)
            v.wait_ge(S.new, 16)
            v.wait_ge(S.tab, 16)
        else:
            v.wait_ge(S["arr%d_%d" % (j, s)], eng)
        v.tensor_copy(off[:, 2 * s:2 * s + 2], blk[:, HALF - 2 + 2 * s:HALF + 2 * s]).then_inc(S.cv, 1)
        v.wait_ge(S.cv, n + 1)
        v.wait_ge(S.sc, n)
        dc = s * (HALF + 4)
        v.tensor_copy(T.win[:, 0:N * R].indirect(off[:, 2 * s:2 * s + 2]), blk[:, dc:dc + NEW]).then_inc(S.sc, 1)
        n += 1

    g.sync.wait_ge(S.sc, n)
    g.sync.dma_start(T.y[:, :], T.win[:, c0:c0 + R]).then_inc(S.out, 16)
    g.sync.wait_ge(S.out, 16)
    g.wait_ge(S.sent, sent[0])
